import numpy as np
import ml_dtypes


def mxq(x, axis, fmt="e4m3"):
    dtype, down = {"e4m3": (ml_dtypes.float8_e4m3fn, 7), "e5m2": (ml_dtypes.float8_e5m2, 14)}[fmt]
    v = np.moveaxis(np.asarray(x, np.float32).astype(ml_dtypes.bfloat16).astype(np.float64), axis, -1)
    blocks = v.reshape(v.shape[:-1] + (-1, 32))
    amax = np.abs(blocks).max(-1, keepdims=True)
    byte = np.maximum(np.where(amax > 0, np.frexp(amax)[1] - 1 + 127, 0) - down, 1)
    scale = np.exp2(byte - 127.0)
    codes = (blocks / scale).astype(np.float32).astype(dtype).astype(np.float64)
    return np.moveaxis((codes * scale).reshape(v.shape), -1, axis)


WIDE = False


def mx_kscale(k):
    if not WIDE:
        return np.ones(k)
    levels = np.array([10, -10, 5, -5, 0])
    if k % 512:
        return np.exp2(np.random.permutation(np.resize(levels, k // 32))).repeat(32)
    a = np.empty((k // 512, 16))
    for p in range(k // 512):
        a[p, :8] = np.random.permutation(np.resize(levels, 8))
        for g in range(8):
            far = levels[np.abs(levels - a[p, g]) >= 10]
            a[p, g + 8] = far[np.random.randint(len(far))]
    return np.exp2(a.ravel()).repeat(32)


def f64(x):
    return np.asarray(x).astype(np.float64)


def striped(idx):
    return np.tile(idx.reshape(-1, 16).T, (8, 1)).astype(np.uint16)


def unstriped(offs):
    return offs[:16].T.reshape(-1).astype(np.int64)


def pack_weight(w):
    k, n = w.shape
    w = f64(np.asarray(w, np.float32).astype(ml_dtypes.bfloat16)).reshape(k // 32, 32, n)
    amax = np.abs(w).max(1)
    byte = np.clip(np.where(amax > 0, np.frexp(amax)[1] - 1 + 127 - 7, 1), 1, 254)
    scaled = (w * np.exp2(127.0 - byte)[:, None, :]).reshape(k, n).astype(np.float32)
    words = np.ascontiguousarray(scaled.reshape(k // 512, 128, 4, n).transpose(0, 1, 3, 2)).astype(ml_dtypes.float8_e4m3fn).view(np.uint8)
    return words, np.ascontiguousarray(byte.astype(np.uint8).reshape(k // 512, 16, n))


def unpack_weight(words, scales):
    g, p, n, _ = words.shape
    vals = np.ascontiguousarray(words).view(ml_dtypes.float8_e4m3fn).astype(np.float64) * np.repeat(np.exp2(scales.astype(np.float64) - 127.0), 8, axis=1)[..., None]
    return vals.transpose(0, 1, 3, 2).reshape(g * 512, n)


def planes(y):
    n, m = y.shape
    v = y.astype(np.float32).astype(ml_dtypes.bfloat16).astype(np.float64).reshape(n // 32, 32, m)
    top = np.abs(v).max(1)
    byte = np.clip(np.where(top > 0, np.frexp(top)[1] - 1 + 127 - 7, 1), 1, 254)
    codes = (v * np.exp2(127.0 - byte)[:, None, :]).reshape(n, m).astype(np.float32).astype(ml_dtypes.float8_e4m3fn).view(np.uint8)
    words = codes.reshape(n // 512, 128, 4, m).transpose(0, 1, 3, 2)
    return np.ascontiguousarray(words), np.ascontiguousarray(byte.astype(np.uint8).reshape(n // 512, 16, m))


def sigmoid(v):
    return 1.0 / (1.0 + np.exp(-np.maximum(v, -700.0)))


K, T, S, N = 512, 2048, 512, 512


def setup_inputs():
    n = np.random.standard_normal
    s = mx_kscale(K)[:, None]
    packed_xT = pack_weight(n((K, T)) * s)
    return {
        "x_words": packed_xT[0],
        "x_scales": packed_xT[1],
        "w0": (n((K, N)) / np.sqrt(3 * K) / s).astype(np.float32),
        "v0": (n((K, N)) / np.sqrt(3 * K) / s).astype(np.float32),
        "w1": (n((K, N)) / np.sqrt(3 * K) / s).astype(np.float32),
        "v1": (n((K, N)) / np.sqrt(3 * K) / s).astype(np.float32),
        "w2": (n((K, N)) / np.sqrt(3 * K) / s).astype(np.float32),
        "v2": (n((K, N)) / np.sqrt(3 * K) / s).astype(np.float32),
        "offs": striped(np.random.permutation(T)[:S]),
        "back1": striped(np.random.permutation(T)[:S]),
        "back2": striped(np.random.permutation(T)[:S]),
    }


def reference(x_words, x_scales, w0, v0, w1, v1, w2, v2, offs, back1, back2):
    xq = unpack_weight(x_words, x_scales)[:, unstriped(offs)]
    x_back1 = unpack_weight(x_words, x_scales)[:, unstriped(back1)]
    x_back2 = unpack_weight(x_words, x_scales)[:, unstriped(back2)]
    f = mxq(f64(w0), 0, "e4m3").T @ xq + mxq(f64(w1), 0, "e4m3").T @ x_back1 + mxq(f64(w2), 0, "e4m3").T @ x_back2
    g = sigmoid(mxq(f64(v0), 0, "e4m3").T @ xq + mxq(f64(v1), 0, "e4m3").T @ x_back1 + mxq(f64(v2), 0, "e4m3").T @ x_back2)
    out_0 = f * g
    return (out_0,) + planes(out_0)

@@ -1,0 +1,179 @@
+from contextlib import ExitStack
+
+import concourse.mybir as mybir
+
+K, T, S, N = 512, 2048, 512, 512
+TAPS = 3
+FLOPS = 2 * TAPS * 2 * K * N * S
+
+F32 = mybir.dt.float32
+BF16 = mybir.dt.bfloat16
+I32 = mybir.dt.int32
+U32 = mybir.dt.uint32
+U16 = mybir.dt.uint16
+U8 = mybir.dt.uint8
+FP8X4 = mybir.dt.float8_e4m3fn_x4
+SIGMOID = mybir.ActivationFunctionType.Sigmoid
+MULT = mybir.AluOpType.mult
+
+P = 128
+PACK = 4
+CHUNKS = (128, 128, 128, 128)
+
+
+def tile_picked_zwave_glu_po_kernel(
+    tc, x_words, x_scales, w0, v0, w1, v1, w2, v2, offs, back1, back2, out_0, out_1, out_2
+):
+    nc = tc.nc
+    with ExitStack() as ctx:
+        keep = ctx.enter_context(tc.tile_pool(name="keep", bufs=1))
+        psum = ctx.enter_context(tc.psum_pool(name="psum", bufs=1))
+
+        lists = []
+        for d, src in enumerate((offs, back1, back2)):
+            lst = keep.tile([P, S // 16], U16, name=f"list{d}")
+            nc.sync.dma_start(lst[:], src)
+            lists.append(lst)
+
+        table_scales = keep.tile([P, T], U8, name="table_scales", align_bytes=64)
+        nc.vector.memset(table_scales[:].bitcast(I32), 0)
+        for q in range(4):
+            nc.scalar.dma_start(
+                out=table_scales[32 * q : 32 * q + 4, :].bitcast(I32),
+                in_=x_scales[0, 4 * q : 4 * q + 4, :].bitcast(I32),
+            )
+        table_words = keep.tile([P, T], U32, name="table_words", align_bytes=64)
+
+        names = ("v0", "v1", "v2", "w0", "w1", "w2")
+        raw = {}
+        for name, src in zip(names, (v0, v1, v2, w0, w1, w2)):
+            raw[name] = keep.tile([P, PACK, N], F32, name=f"raw_{name}", align_bytes=64)
+            nc.sync.dma_start(out=raw[name][:], in_=src.rearrange("(p j) c -> p j c", j=PACK))
+            if name == "v0":
+                nc.sync.dma_start(
+                    out=table_words[:].bitcast(I32),
+                    in_=x_words[0].rearrange("p c r -> p (c r)").bitcast(I32),
+                )
+
+        warm_in = keep.tile([P, 1], F32, name="warm_in")
+        warm_out = keep.tile([P, 1], F32, name="warm_out")
+        nc.vector.memset(warm_in[:], 0.0)
+        nc.scalar.activation(warm_out[:], warm_in[:], SIGMOID)
+
+        picked_words, picked_scales = [], []
+        for d in range(TAPS):
+            ps = keep.tile([P, S], U8, name=f"picked_scales{d}", align_bytes=64)
+            nc.vector.tensor_copy(ps[:], table_scales[:].indirect(lists[d][:]))
+            picked_scales.append(ps)
+        for d in range(TAPS):
+            pw = keep.tile([P, S], U32, name=f"picked_words{d}", align_bytes=64)
+            nc.vector.tensor_copy(pw[:], table_words[:].indirect(lists[d][:]))
+            picked_words.append(pw)
+
+        staged, codes, scales = {}, {}, {}
+        for name in names:
+            for u in range(2):
+                staged[name, u] = keep.tile([P, 2, P, PACK], BF16, name=f"staged_{name}_{u}", align_bytes=64)
+                codes[name, u] = keep.tile([P, 2 * P], U32, name=f"codes_{name}_{u}", align_bytes=64)
+                scales[name, u] = keep.tile([P, 2 * P], U8, name=f"scales_{name}_{u}", align_bytes=64)
+
+        def cast(copy, name, u, m0=0, m1=P):
+            src = raw[name][:].rearrange("p j (m u e) -> p u m j e", u=2, e=2)
+            dst = staged[name, u][:].rearrange("p e m j -> p m j e")
+            copy(out=dst[:, m0:m1, :, :], in_=src[:, u, m0:m1, :, :])
+
+        def quantise(name, u):
+            nc.vector.quantize_mx(
+                out=codes[name, u][:].bitcast(FP8X4),
+                scales=scales[name, u][:],
+                in_=staged[name, u][:].rearrange("p e m j -> p (e m j)"),
+            )
+
+        def multiply(acc, name, d, u):
+            for e in range(2):
+                cols = slice(e * P, (e + 1) * P)
+                nc.tensor.matmul_mx(
+                    out=acc[2 * u + e][:],
+                    lhsT=codes[name, u][:, cols].bitcast(FP8X4),
+                    lhsT_scale=scales[name, u][:, cols],
+                    rhs=picked_words[d][:].bitcast(FP8X4),
+                    rhs_scale=picked_scales[d][:],
+                    start=(d == 0),
+                    stop=(d == TAPS - 1),
+                )
+
+        on_s, on_v = nc.scalar.copy, nc.vector.tensor_copy
+        g_acc = [psum.tile([P, S], F32, name=f"g_acc{t}") for t in range(PACK)]
+        f_acc = [psum.tile([P, S], F32, name=f"f_acc{t}") for t in range(PACK)]
+        gate = [keep.tile([P, S], F32, name=f"gate{t}") for t in range(PACK)]
+
+        plan = {"v0": (on_s, on_s), "v1": (on_s, on_s), "v2": (on_s, on_v), "w0": (on_v, on_v), "w1": (on_v, on_s)}
+        for d in range(TAPS):
+            name = f"v{d}"
+            for u in range(2):
+                cast(plan[name][u], name, u)
+            for u in range(2):
+                quantise(name, u)
+                multiply(g_acc, name, d, u)
+        for u in range(2):
+            cast(plan["w0"][u], "w0", u)
+        for t in range(PACK):
+            nc.scalar.activation(gate[t][:], g_acc[t][:], SIGMOID)
+        for u in range(2):
+            quantise("w0", u)
+            multiply(f_acc, "w0", 0, u)
+        for u in range(2):
+            cast(plan["w1"][u], "w1", u)
+        for u in range(2):
+            quantise("w1", u)
+            multiply(f_acc, "w1", 1, u)
+        cast(on_v, "w2", 0)
+        cast(on_v, "w2", 1, 0, 32)
+        cast(on_s, "w2", 1, 32, P)
+        for u in range(2):
+            quantise("w2", u)
+            multiply(f_acc, "w2", 2, u)
+
+        y_codes = keep.tile([P, S], U32, name="y_codes", align_bytes=64)
+        y_scales = keep.tile([P, S], U8, name="y_scales", align_bytes=64)
+        out_rows = out_0.rearrange("(p t) j -> p t j", t=PACK)
+        out_words = out_1[0].rearrange("p c r -> p (c r)").bitcast(I32)
+        rounded = []
+        c0 = 0
+        spans = []
+        for c, width in enumerate(CHUNKS):
+            spans.append(slice(c0, c0 + width))
+            c0 = c0 + width
+
+        def finish(c):
+            cols = spans[c]
+            nc.vector.quantize_mx(
+                out=y_codes[:, cols].bitcast(FP8X4),
+                scales=y_scales[:, cols],
+                in_=rounded[c][:].rearrange("p c t -> p (c t)"),
+            )
+
+        for c, width in enumerate(CHUNKS):
+            cols = spans[c]
+            y = keep.tile([P, PACK, width], F32, name=f"y{c}", align_bytes=64)
+            for t in range(PACK):
+                nc.vector.tensor_tensor(y[:, t, :], f_acc[t][:, cols], gate[t][:, cols], MULT)
+            nc.sync.dma_start(out=out_rows[:, :, cols], in_=y[:])
+            yb = keep.tile([P, width, PACK], BF16, name=f"rounded{c}", align_bytes=64)
+            nc.scalar.copy(
+                out=yb[:].rearrange("p (c i) t -> p c t i", i=2),
+                in_=y[:].rearrange("p t (c i) -> p c t i", i=2),
+            )
+            rounded.append(yb)
+            if c >= 1:
+                finish(c - 1)
+            if c == 2:
+                nc.sync.dma_start(out=out_words[:, 0:256], in_=y_codes[:, 0:256].bitcast(I32))
+        finish(len(CHUNKS) - 1)
+        nc.sync.dma_start(out=out_words[:, 256:512], in_=y_codes[:, 256:512].bitcast(I32))
+        for q in range(4):
+            queue = nc.sync if q % 2 == 0 else nc.scalar
+            queue.dma_start(
+                out=out_2[0, 4 * q : 4 * q + 4, :].bitcast(I32),
+                in_=y_scales[32 * q : 32 * q + 4, :].bitcast(I32),
+            )

@@ -36,9 +36,10 @@ def tile_picked_zwave_glu_po_kernel(
             lists.append(lst)
 
         table_scales = keep.tile([P, T], U8, name="table_scales", align_bytes=64)
-        nc.vector.memset(table_scales[:].bitcast(I32), 0)
+        nc.vector.memset(table_scales[:, : T // 2].bitcast(I32), 0)
+        nc.gpsimd.memset(table_scales[:, T // 2 :].bitcast(I32), 0)
         for q in range(4):
-            nc.scalar.dma_start(
+            nc.sync.dma_start(
                 out=table_scales[32 * q : 32 * q + 4, :].bitcast(I32),
                 in_=x_scales[0, 4 * q : 4 * q + 4, :].bitcast(I32),
             )
@@ -46,7 +47,7 @@ def tile_picked_zwave_glu_po_kernel(
 
         names = ("v0", "v1", "v2", "w0", "w1", "w2")
         raw = {}
-        for name, src in zip(names, (v0, v1, v2, w0, w1, w2)):
+        for name, src in zip(names[:-1], (v0, v1, v2, w0, w1)):
             raw[name] = keep.tile([P, PACK, N], F32, name=f"raw_{name}", align_bytes=64)
             nc.sync.dma_start(out=raw[name][:], in_=src.rearrange("(p j) c -> p j c", j=PACK))
             if name == "v0":
@@ -54,6 +55,14 @@ def tile_picked_zwave_glu_po_kernel(
                     out=table_words[:].bitcast(I32),
                     in_=x_words[0].rearrange("p c r -> p (c r)").bitcast(I32),
                 )
+
+        last_raw = []
+        for h in range(2):
+            part = keep.tile([P, PACK, N // 2], F32, name=f"raw_w2_{h}", align_bytes=64)
+            nc.sync.dma_start(
+                out=part[:], in_=w2.rearrange("(p j) c -> p j c", j=PACK)[:, :, h * (N // 2) : (h + 1) * (N // 2)]
+            )
+            last_raw.append(part)
 
         warm_in = keep.tile([P, 1], F32, name="warm_in")
         warm_out = keep.tile([P, 1], F32, name="warm_out")
@@ -73,7 +82,8 @@ def tile_picked_zwave_glu_po_kernel(
         staged, codes, scales = {}, {}, {}
         for name in names:
             for u in range(2):
-                staged[name, u] = keep.tile([P, 2, P, PACK], BF16, name=f"staged_{name}_{u}", align_bytes=64)
+                if name != "w2":
+                    staged[name, u] = keep.tile([P, 2, P, PACK], BF16, name=f"staged_{name}_{u}", align_bytes=64)
                 codes[name, u] = keep.tile([P, 2 * P], U32, name=f"codes_{name}_{u}", align_bytes=64)
                 scales[name, u] = keep.tile([P, 2 * P], U8, name=f"scales_{name}_{u}", align_bytes=64)
 
@@ -107,70 +117,86 @@ def tile_picked_zwave_glu_po_kernel(
         f_acc = [psum.tile([P, S], F32, name=f"f_acc{t}") for t in range(PACK)]
         gate = [keep.tile([P, S], F32, name=f"gate{t}") for t in range(PACK)]
 
-        plan = {"v0": (on_s, on_s), "v1": (on_s, on_s), "v2": (on_s, on_v), "w0": (on_v, on_v), "w1": (on_v, on_s)}
         for d in range(TAPS):
             name = f"v{d}"
-            for u in range(2):
-                cast(plan[name][u], name, u)
-            for u in range(2):
+            cast(on_s, name, 0)
+            cast(on_v if d == TAPS - 1 else on_s, name, 1)
+            for u in ((1, 0) if d == TAPS - 1 else (0, 1)):
                 quantise(name, u)
                 multiply(g_acc, name, d, u)
-        for u in range(2):
-            cast(plan["w0"][u], "w0", u)
-        for t in range(PACK):
+        for t in (2, 3, 0, 1):
             nc.scalar.activation(gate[t][:], g_acc[t][:], SIGMOID)
+        for u in range(2):
+            cast(on_v, "w0", u)
         for u in range(2):
             quantise("w0", u)
             multiply(f_acc, "w0", 0, u)
-        for u in range(2):
-            cast(plan["w1"][u], "w1", u)
-        for u in range(2):
+        cast(on_s, "w1", 0)
+        cast(on_v, "w1", 1)
+        for u in (1, 0):
             quantise("w1", u)
             multiply(f_acc, "w1", 1, u)
-        cast(on_v, "w2", 0)
-        cast(on_v, "w2", 1, 0, 32)
-        cast(on_s, "w2", 1, 32, P)
-        for u in range(2):
-            quantise("w2", u)
-            multiply(f_acc, "w2", 2, u)
+        for h in range(2):
+            halves = []
+            for u in range(2):
+                st = keep.tile([P, 2, P // 2, PACK], BF16, name=f"staged_w2_{h}_{u}", align_bytes=64)
+                src = last_raw[h][:].rearrange("p j (m u e) -> p u m j e", u=2, e=2)
+                (on_v if u == 0 else on_s)(out=st[:].rearrange("p e m j -> p m j e"), in_=src[:, u, :, :, :])
+                halves.append(st)
+            for u in range(2):
+                for e in range(2):
+                    cols = slice(e * P + h * (P // 2), e * P + (h + 1) * (P // 2))
+                    nc.vector.quantize_mx(
+                        out=codes["w2", u][:, cols].bitcast(FP8X4),
+                        scales=scales["w2", u][:, cols],
+                        in_=halves[u][:, e, :, :].rearrange("p m j -> p (m j)"),
+                    )
+                if h == 1:
+                    multiply(f_acc, "w2", 2, u)
 
         y_codes = keep.tile([P, S], U32, name="y_codes", align_bytes=64)
         y_scales = keep.tile([P, S], U8, name="y_scales", align_bytes=64)
         out_rows = out_0.rearrange("(p t) j -> p t j", t=PACK)
         out_words = out_1[0].rearrange("p c r -> p (c r)").bitcast(I32)
-        rounded = []
-        c0 = 0
-        spans = []
-        for c, width in enumerate(CHUNKS):
-            spans.append(slice(c0, c0 + width))
-            c0 = c0 + width
+        HALF, QUARTER = S // 2, S // 4
+        ys = [keep.tile([P, PACK, HALF], F32, name=f"y{h}", align_bytes=64) for h in range(2)]
+        rounded = [keep.tile([P, QUARTER, PACK], BF16, name=f"rounded{c}", align_bytes=64) for c in range(4)]
+
+        def gate_half(h):
+            cols = slice(h * HALF, (h + 1) * HALF)
+            for t in range(PACK):
+                nc.vector.tensor_tensor(ys[h][:, t, :], f_acc[t][:, cols], gate[t][:, cols], MULT)
+                if t % 2 == 1:
+                    nc.sync.dma_start(out=out_rows[:, t - 1 : t + 1, cols], in_=ys[h][:, t - 1 : t + 1, :])
+
+        def round_quarter(copy, c):
+            h, part = divmod(c, 2)
+            src = ys[h][:, :, part * QUARTER : (part + 1) * QUARTER]
+            copy(
+                out=rounded[c][:].rearrange("p (c i) t -> p c t i", i=2),
+                in_=src.rearrange("p t (c i) -> p c t i", i=2),
+            )
 
         def finish(c):
-            cols = spans[c]
+            cols = slice(c * QUARTER, (c + 1) * QUARTER)
             nc.vector.quantize_mx(
                 out=y_codes[:, cols].bitcast(FP8X4),
                 scales=y_scales[:, cols],
                 in_=rounded[c][:].rearrange("p c t -> p (c t)"),
             )
 
-        for c, width in enumerate(CHUNKS):
-            cols = spans[c]
-            y = keep.tile([P, PACK, width], F32, name=f"y{c}", align_bytes=64)
-            for t in range(PACK):
-                nc.vector.tensor_tensor(y[:, t, :], f_acc[t][:, cols], gate[t][:, cols], MULT)
-            nc.sync.dma_start(out=out_rows[:, :, cols], in_=y[:])
-            yb = keep.tile([P, width, PACK], BF16, name=f"rounded{c}", align_bytes=64)
-            nc.scalar.copy(
-                out=yb[:].rearrange("p (c i) t -> p c t i", i=2),
-                in_=y[:].rearrange("p t (c i) -> p c t i", i=2),
-            )
-            rounded.append(yb)
-            if c >= 1:
-                finish(c - 1)
-            if c == 2:
-                nc.sync.dma_start(out=out_words[:, 0:256], in_=y_codes[:, 0:256].bitcast(I32))
-        finish(len(CHUNKS) - 1)
-        nc.sync.dma_start(out=out_words[:, 256:512], in_=y_codes[:, 256:512].bitcast(I32))
+        gate_half(0)
+        round_quarter(on_s, 0)
+        round_quarter(on_s, 1)
+        gate_half(1)
+        round_quarter(on_s, 2)
+        finish(0)
+        round_quarter(on_v, 3)
+        finish(1)
+        nc.sync.dma_start(out=out_words[:, 0:HALF], in_=y_codes[:, 0:HALF].bitcast(I32))
+        finish(3)
+        finish(2)
+        nc.sync.dma_start(out=out_words[:, HALF:S], in_=y_codes[:, HALF:S].bitcast(I32))
         for q in range(4):
             queue = nc.sync if q % 2 == 0 else nc.scalar
             queue.dma_start(

@@ -29,32 +29,27 @@ def tile_picked_zwave_glu_po_kernel(
         keep = ctx.enter_context(tc.tile_pool(name="keep", bufs=1))
         psum = ctx.enter_context(tc.psum_pool(name="psum", bufs=1))
 
-        lists = []
-        for d, src in enumerate((offs, back1, back2)):
-            lst = keep.tile([P, S // 16], U16, name=f"list{d}")
-            nc.sync.dma_start(lst[:], src)
-            lists.append(lst)
-
+        lists = [keep.tile([P, S // 16], U16, name=f"list{d}") for d in range(TAPS)]
+        table_words = keep.tile([P, T], U32, name="table_words", align_bytes=64)
         table_scales = keep.tile([P, T], U8, name="table_scales", align_bytes=64)
-        nc.vector.memset(table_scales[:, : T // 2].bitcast(I32), 0)
-        nc.gpsimd.memset(table_scales[:, T // 2 :].bitcast(I32), 0)
+        words_in = x_words[0].rearrange("p c r -> p (c r)").bitcast(I32)
+        nc.vector.memset(table_scales[:].bitcast(I32), 0)
+        nc.sync.dma_start(lists[0][:], offs)
+        nc.sync.dma_start(out=table_words[:, : T // 2].bitcast(I32), in_=words_in[:, : T // 2])
+        nc.sync.dma_start(lists[1][:], back1)
+        nc.sync.dma_start(lists[2][:], back2)
         for q in range(4):
             nc.sync.dma_start(
                 out=table_scales[32 * q : 32 * q + 4, :].bitcast(I32),
                 in_=x_scales[0, 4 * q : 4 * q + 4, :].bitcast(I32),
             )
-        table_words = keep.tile([P, T], U32, name="table_words", align_bytes=64)
+        nc.sync.dma_start(out=table_words[:, T // 2 :].bitcast(I32), in_=words_in[:, T // 2 :])
 
         names = ("v0", "v1", "v2", "w0", "w1", "w2")
         raw = {}
         for name, src in zip(names[:-1], (v0, v1, v2, w0, w1)):
             raw[name] = keep.tile([P, PACK, N], F32, name=f"raw_{name}", align_bytes=64)
             nc.sync.dma_start(out=raw[name][:], in_=src.rearrange("(p j) c -> p j c", j=PACK))
-            if name == "v0":
-                nc.sync.dma_start(
-                    out=table_words[:].bitcast(I32),
-                    in_=x_words[0].rearrange("p c r -> p (c r)").bitcast(I32),
-                )
 
         last_raw = []
         for h in range(2):
@@ -82,8 +77,7 @@ def tile_picked_zwave_glu_po_kernel(
         staged, codes, scales = {}, {}, {}
         for name in names:
             for u in range(2):
-                if name != "w2":
-                    staged[name, u] = keep.tile([P, 2, P, PACK], BF16, name=f"staged_{name}_{u}", align_bytes=64)
+                staged[name, u] = keep.tile([P, 2, P, PACK], BF16, name=f"staged_{name}_{u}", align_bytes=64)
                 codes[name, u] = keep.tile([P, 2 * P], U32, name=f"codes_{name}_{u}", align_bytes=64)
                 scales[name, u] = keep.tile([P, 2 * P], U8, name=f"scales_{name}_{u}", align_bytes=64)
 
@@ -115,44 +109,35 @@ def tile_picked_zwave_glu_po_kernel(
         on_s, on_v = nc.scalar.copy, nc.vector.tensor_copy
         g_acc = [psum.tile([P, S], F32, name=f"g_acc{t}") for t in range(PACK)]
         f_acc = [psum.tile([P, S], F32, name=f"f_acc{t}") for t in range(PACK)]
-        gate = [keep.tile([P, S], F32, name=f"gate{t}") for t in range(PACK)]
+        gate = [raw["w0"][:, t, :] for t in range(PACK)]
 
         for d in range(TAPS):
             name = f"v{d}"
-            cast(on_s, name, 0)
-            cast(on_v if d == TAPS - 1 else on_s, name, 1)
-            for u in ((1, 0) if d == TAPS - 1 else (0, 1)):
+            for u in range(2):
+                cast(on_s, name, u)
+            for u in range(2):
                 quantise(name, u)
                 multiply(g_acc, name, d, u)
-        for t in (2, 3, 0, 1):
-            nc.scalar.activation(gate[t][:], g_acc[t][:], SIGMOID)
-        for u in range(2):
-            cast(on_v, "w0", u)
-        for u in range(2):
+        cast(on_s, "w0", 0)
+        cast(on_v, "w0", 1)
+        for u in (1, 0):
             quantise("w0", u)
             multiply(f_acc, "w0", 0, u)
-        cast(on_s, "w1", 0)
-        cast(on_v, "w1", 1)
-        for u in (1, 0):
+        for t in range(PACK):
+            nc.scalar.activation(gate[t], g_acc[t][:], SIGMOID)
+        for u in range(2):
+            cast(on_v, "w1", u)
+        for u in range(2):
             quantise("w1", u)
             multiply(f_acc, "w1", 1, u)
         for h in range(2):
-            halves = []
-            for u in range(2):
-                st = keep.tile([P, 2, P // 2, PACK], BF16, name=f"staged_w2_{h}_{u}", align_bytes=64)
-                src = last_raw[h][:].rearrange("p j (m u e) -> p u m j e", u=2, e=2)
-                (on_v if u == 0 else on_s)(out=st[:].rearrange("p e m j -> p m j e"), in_=src[:, u, :, :, :])
-                halves.append(st)
-            for u in range(2):
-                for e in range(2):
-                    cols = slice(e * P + h * (P // 2), e * P + (h + 1) * (P // 2))
-                    nc.vector.quantize_mx(
-                        out=codes["w2", u][:, cols].bitcast(FP8X4),
-                        scales=scales["w2", u][:, cols],
-                        in_=halves[u][:, e, :, :].rearrange("p m j -> p (m j)"),
-                    )
-                if h == 1:
-                    multiply(f_acc, "w2", 2, u)
+            src = last_raw[h][:].rearrange("p j (m u e) -> p u m j e", u=2, e=2)
+            for u, copy in enumerate((on_v, on_s)):
+                dst = staged["w2", u][:].rearrange("p e m j -> p m j e")
+                copy(out=dst[:, h * (P // 2) : (h + 1) * (P // 2), :, :], in_=src[:, u, :, :, :])
+        for u in range(2):
+            quantise("w2", u)
+            multiply(f_acc, "w2", 2, u)
 
         y_codes = keep.tile([P, S], U32, name="y_codes", align_bytes=64)
         y_scales = keep.tile([P, S], U8, name="y_scales", align_bytes=64)

@@ -18,7 +18,7 @@ MULT = mybir.AluOpType.mult
 
 P = 128
 PACK = 4
-CHUNKS = (128, 128, 128, 128)
+HALF, QUARTER = S // 2, S // 4
 
 
 def tile_picked_zwave_glu_po_kernel(
@@ -43,17 +43,18 @@ def tile_picked_zwave_glu_po_kernel(
                 out=table_scales[32 * q : 32 * q + 4, :].bitcast(I32),
                 in_=x_scales[0, 4 * q : 4 * q + 4, :].bitcast(I32),
             )
-        nc.sync.dma_start(out=table_words[:, T // 2 :].bitcast(I32), in_=words_in[:, T // 2 :])
 
         names = ("v0", "v1", "v2", "w0", "w1", "w2")
         raw = {}
         for name, src in zip(names[:-1], (v0, v1, v2, w0, w1)):
-            raw[name] = keep.tile([P, PACK, N], F32, name=f"raw_{name}", align_bytes=64)
+            raw[name] = keep.tile([P, PACK, N], F32, name=f"raw_{name}", tag=f"raw_{name}", align_bytes=64)
             nc.sync.dma_start(out=raw[name][:], in_=src.rearrange("(p j) c -> p j c", j=PACK))
+            if name == "v0":
+                nc.sync.dma_start(out=table_words[:, T // 2 :].bitcast(I32), in_=words_in[:, T // 2 :])
 
         last_raw = []
         for h in range(2):
-            part = keep.tile([P, PACK, N // 2], F32, name=f"raw_w2_{h}", align_bytes=64)
+            part = keep.tile([P, PACK, N // 2], F32, name=f"raw_w2_{h}", tag=f"raw_w2_{h}", align_bytes=64)
             nc.sync.dma_start(
                 out=part[:], in_=w2.rearrange("(p j) c -> p j c", j=PACK)[:, :, h * (N // 2) : (h + 1) * (N // 2)]
             )
@@ -69,22 +70,29 @@ def tile_picked_zwave_glu_po_kernel(
             ps = keep.tile([P, S], U8, name=f"picked_scales{d}", align_bytes=64)
             nc.vector.tensor_copy(ps[:], table_scales[:].indirect(lists[d][:]))
             picked_scales.append(ps)
-        for d in range(TAPS):
-            pw = keep.tile([P, S], U32, name=f"picked_words{d}", align_bytes=64)
+
+        def gather_words(d, tag):
+            pw = keep.tile([P, S], U32, name=f"picked_words{d}", tag=tag, align_bytes=64)
             nc.vector.tensor_copy(pw[:], table_words[:].indirect(lists[d][:]))
             picked_words.append(pw)
+
+        gather_words(0, "picked_words0")
 
         staged, codes, scales = {}, {}, {}
         for name in names:
             for u in range(2):
-                staged[name, u] = keep.tile([P, 2, P, PACK], BF16, name=f"staged_{name}_{u}", align_bytes=64)
+                staged[name, u] = keep.tile([P, 2, P, PACK], BF16, name=f"staged_{name}_{u}", tag=f"staged_{name}_{u}", align_bytes=64)
                 codes[name, u] = keep.tile([P, 2 * P], U32, name=f"codes_{name}_{u}", align_bytes=64)
                 scales[name, u] = keep.tile([P, 2 * P], U8, name=f"scales_{name}_{u}", align_bytes=64)
 
-        def cast(copy, name, u, m0=0, m1=P):
+        def cast(copy, name, u):
             src = raw[name][:].rearrange("p j (m u e) -> p u m j e", u=2, e=2)
-            dst = staged[name, u][:].rearrange("p e m j -> p m j e")
-            copy(out=dst[:, m0:m1, :, :], in_=src[:, u, m0:m1, :, :])
+            copy(out=staged[name, u][:].rearrange("p e m j -> p m j e"), in_=src[:, u, :, :, :])
+
+        def cast_last(copy, h, u):
+            src = last_raw[h][:].rearrange("p j (m u e) -> p u m j e", u=2, e=2)
+            dst = staged["w2", u][:].rearrange("p e m j -> p m j e")
+            copy(out=dst[:, h * (P // 2) : (h + 1) * (P // 2), :, :], in_=src[:, u, :, :, :])
 
         def quantise(name, u):
             nc.vector.quantize_mx(
@@ -93,66 +101,90 @@ def tile_picked_zwave_glu_po_kernel(
                 in_=staged[name, u][:].rearrange("p e m j -> p (e m j)"),
             )
 
-        def multiply(acc, name, d, u):
+        def quantise_last(h, u, e):
+            cols = slice(e * P + h * (P // 2), e * P + (h + 1) * (P // 2))
+            nc.vector.quantize_mx(
+                out=codes["w2", u][:, cols].bitcast(FP8X4),
+                scales=scales["w2", u][:, cols],
+                in_=staged["w2", u][:, e, h * (P // 2) : (h + 1) * (P // 2), :].rearrange("p m j -> p (m j)"),
+            )
+
+        def multiply(out, name, d, u, e, frames, start, stop):
+            cols = slice(e * P, (e + 1) * P)
+            nc.tensor.matmul_mx(
+                out=out,
+                lhsT=codes[name, u][:, cols].bitcast(FP8X4),
+                lhsT_scale=scales[name, u][:, cols],
+                rhs=picked_words[d][:, frames].bitcast(FP8X4),
+                rhs_scale=picked_scales[d][:, frames],
+                start=start,
+                stop=stop,
+            )
+
+        def multiply_half(acc, name, d, u, h):
             for e in range(2):
-                cols = slice(e * P, (e + 1) * P)
-                nc.tensor.matmul_mx(
-                    out=acc[2 * u + e][:],
-                    lhsT=codes[name, u][:, cols].bitcast(FP8X4),
-                    lhsT_scale=scales[name, u][:, cols],
-                    rhs=picked_words[d][:].bitcast(FP8X4),
-                    rhs_scale=picked_scales[d][:],
-                    start=(d == 0),
-                    stop=(d == TAPS - 1),
+                multiply(
+                    acc[h][u][:, e, :], name, d, u, e, slice(h * HALF, (h + 1) * HALF),
+                    d == 0 and e == 0, d == TAPS - 1 and e == 1,
                 )
 
+        def multiply_all(acc, name, d, u):
+            for h in range(2):
+                multiply_half(acc, name, d, u, h)
+
+        def gates(h, tag):
+            gate = keep.tile([P, PACK, HALF], F32, name=f"gate{h}", tag=tag, align_bytes=64)
+            for u in range(2):
+                nc.scalar.activation(gate[:, 2 * u : 2 * u + 2, :], g_acc[h][u][:], SIGMOID)
+            return gate
+
         on_s, on_v = nc.scalar.copy, nc.vector.tensor_copy
-        g_acc = [psum.tile([P, S], F32, name=f"g_acc{t}") for t in range(PACK)]
-        f_acc = [psum.tile([P, S], F32, name=f"f_acc{t}") for t in range(PACK)]
-        gate = [raw["w0"][:, t, :] for t in range(PACK)]
+        g_acc = [[psum.tile([P, 2, HALF], F32, name=f"g_acc{h}_{u}") for u in range(2)] for h in range(2)]
+        f_acc = [[psum.tile([P, 2, HALF], F32, name=f"f_acc{h}_{u}") for u in range(2)] for h in range(2)]
 
         for d in range(TAPS):
             name = f"v{d}"
-            for u in range(2):
-                cast(on_s, name, u)
+            cast(on_s, name, 0)
+            cast(on_v if d == TAPS - 1 else on_s, name, 1)
             for u in range(2):
                 quantise(name, u)
-                multiply(g_acc, name, d, u)
-        cast(on_s, "w0", 0)
-        cast(on_v, "w0", 1)
-        for u in (1, 0):
-            quantise("w0", u)
-            multiply(f_acc, "w0", 0, u)
-        for t in range(PACK):
-            nc.scalar.activation(gate[t], g_acc[t][:], SIGMOID)
-        for u in range(2):
-            cast(on_v, "w1", u)
-        for u in range(2):
-            quantise("w1", u)
-            multiply(f_acc, "w1", 1, u)
+                multiply_all(g_acc, name, d, u)
+                if d == 0:
+                    gather_words(u + 1, f"staged_v0_{u}")
+        gate = []
+        for d in range(TAPS - 1):
+            name = f"w{d}"
+            cast(on_v, name, 1)
+            cast(on_s, name, 0)
+            for u in (1, 0):
+                quantise(name, u)
+                multiply_all(f_acc, name, d, u)
+            if d == 0:
+                gate.append(gates(0, "raw_w0"))
         for h in range(2):
-            src = last_raw[h][:].rearrange("p j (m u e) -> p u m j e", u=2, e=2)
-            for u, copy in enumerate((on_v, on_s)):
-                dst = staged["w2", u][:].rearrange("p e m j -> p m j e")
-                copy(out=dst[:, h * (P // 2) : (h + 1) * (P // 2), :, :], in_=src[:, u, :, :, :])
-        for u in range(2):
-            quantise("w2", u)
-            multiply(f_acc, "w2", 2, u)
+            cast_last(on_v, h, 0)
+            cast_last(on_s, h, 1)
+            for u in range(2):
+                for e in range(2):
+                    quantise_last(h, u, e)
+        gate.append(gates(1, "raw_w2_1"))
+        for h in range(2):
+            for u in range(2):
+                multiply_half(f_acc, "w2", TAPS - 1, u, h)
 
         y_codes = keep.tile([P, S], U32, name="y_codes", align_bytes=64)
         y_scales = keep.tile([P, S], U8, name="y_scales", align_bytes=64)
         out_rows = out_0.rearrange("(p t) j -> p t j", t=PACK)
         out_words = out_1[0].rearrange("p c r -> p (c r)").bitcast(I32)
-        HALF, QUARTER = S // 2, S // 4
         ys = [keep.tile([P, PACK, HALF], F32, name=f"y{h}", align_bytes=64) for h in range(2)]
         rounded = [keep.tile([P, QUARTER, PACK], BF16, name=f"rounded{c}", align_bytes=64) for c in range(4)]
 
         def gate_half(h):
             cols = slice(h * HALF, (h + 1) * HALF)
-            for t in range(PACK):
-                nc.vector.tensor_tensor(ys[h][:, t, :], f_acc[t][:, cols], gate[t][:, cols], MULT)
-                if t % 2 == 1:
-                    nc.sync.dma_start(out=out_rows[:, t - 1 : t + 1, cols], in_=ys[h][:, t - 1 : t + 1, :])
+            for u in range(2):
+                pair = slice(2 * u, 2 * u + 2)
+                nc.vector.tensor_tensor(ys[h][:, pair, :], f_acc[h][u][:], gate[h][:, pair, :], MULT)
+                nc.sync.dma_start(out=out_rows[:, pair, cols], in_=ys[h][:, pair, :])
 
         def round_quarter(copy, c):
             h, part = divmod(c, 2)

@@ -38,10 +38,10 @@ def tile_picked_zwave_glu_po_kernel(
         nc.sync.dma_start(out=table_words[:, : T // 2].bitcast(I32), in_=words_in[:, : T // 2])
         nc.sync.dma_start(lists[1][:], back1)
         nc.sync.dma_start(lists[2][:], back2)
-        for q in range(4):
+        for r in range(4):
             nc.sync.dma_start(
-                out=table_scales[32 * q : 32 * q + 4, :].bitcast(I32),
-                in_=x_scales[0, 4 * q : 4 * q + 4, :].bitcast(I32),
+                out=table_scales[r:P:32, :].bitcast(I32),
+                in_=x_scales[0, r:16:4, :].bitcast(I32),
             )
 
         names = ("v0", "v1", "v2", "w0", "w1", "w2")

@@ -34,10 +34,9 @@ def tile_picked_zwave_glu_po_kernel(
         table_scales = keep.tile([P, T], U8, name="table_scales", align_bytes=64)
         words_in = x_words[0].rearrange("p c r -> p (c r)").bitcast(I32)
         nc.vector.memset(table_scales[:].bitcast(I32), 0)
-        nc.sync.dma_start(lists[0][:], offs)
         nc.sync.dma_start(out=table_words[:, : T // 2].bitcast(I32), in_=words_in[:, : T // 2])
+        nc.sync.dma_start(lists[0][:], offs)
         nc.sync.dma_start(lists[1][:], back1)
-        nc.sync.dma_start(lists[2][:], back2)
         for r in range(4):
             nc.sync.dma_start(
                 out=table_scales[r:P:32, :].bitcast(I32),
@@ -50,6 +49,7 @@ def tile_picked_zwave_glu_po_kernel(
             raw[name] = keep.tile([P, PACK, N], F32, name=f"raw_{name}", tag=f"raw_{name}", align_bytes=64)
             nc.sync.dma_start(out=raw[name][:], in_=src.rearrange("(p j) c -> p j c", j=PACK))
             if name == "v0":
+                nc.sync.dma_start(lists[2][:], back2)
                 nc.sync.dma_start(out=table_words[:, T // 2 :].bitcast(I32), in_=words_in[:, T // 2 :])
 
         last_raw = []

@@ -44,21 +44,18 @@ def tile_picked_zwave_glu_po_kernel(
             )
 
         names = ("v0", "v1", "v2", "w0", "w1", "w2")
+        pieces = {"v0": 1, "v1": 1, "v2": 1, "w0": 1, "w1": 2, "w2": 2}
         raw = {}
-        for name, src in zip(names[:-1], (v0, v1, v2, w0, w1)):
-            raw[name] = keep.tile([P, PACK, N], F32, name=f"raw_{name}", tag=f"raw_{name}", align_bytes=64)
-            nc.sync.dma_start(out=raw[name][:], in_=src.rearrange("(p j) c -> p j c", j=PACK))
+        for name, src in zip(names, (v0, v1, v2, w0, w1, w2)):
+            width = N // pieces[name]
+            for h in range(pieces[name]):
+                raw[name, h] = keep.tile([P, PACK, width], F32, name=f"raw_{name}_{h}", tag=f"raw_{name}_{h}", align_bytes=64)
+                nc.sync.dma_start(
+                    out=raw[name, h][:], in_=src.rearrange("(p j) c -> p j c", j=PACK)[:, :, h * width : (h + 1) * width]
+                )
             if name == "v0":
                 nc.sync.dma_start(lists[2][:], back2)
                 nc.sync.dma_start(out=table_words[:, T // 2 :].bitcast(I32), in_=words_in[:, T // 2 :])
-
-        last_raw = []
-        for h in range(2):
-            part = keep.tile([P, PACK, N // 2], F32, name=f"raw_w2_{h}", tag=f"raw_w2_{h}", align_bytes=64)
-            nc.sync.dma_start(
-                out=part[:], in_=w2.rearrange("(p j) c -> p j c", j=PACK)[:, :, h * (N // 2) : (h + 1) * (N // 2)]
-            )
-            last_raw.append(part)
 
         warm_in = keep.tile([P, 1], F32, name="warm_in")
         warm_out = keep.tile([P, 1], F32, name="warm_out")
@@ -85,14 +82,11 @@ def tile_picked_zwave_glu_po_kernel(
                 codes[name, u] = keep.tile([P, 2 * P], U32, name=f"codes_{name}_{u}", align_bytes=64)
                 scales[name, u] = keep.tile([P, 2 * P], U8, name=f"scales_{name}_{u}", align_bytes=64)
 
-        def cast(copy, name, u):
-            src = raw[name][:].rearrange("p j (m u e) -> p u m j e", u=2, e=2)
-            copy(out=staged[name, u][:].rearrange("p e m j -> p m j e"), in_=src[:, u, :, :, :])
-
-        def cast_last(copy, h, u):
-            src = last_raw[h][:].rearrange("p j (m u e) -> p u m j e", u=2, e=2)
-            dst = staged["w2", u][:].rearrange("p e m j -> p m j e")
-            copy(out=dst[:, h * (P // 2) : (h + 1) * (P // 2), :, :], in_=src[:, u, :, :, :])
+        def cast(copy, name, u, h=0):
+            width = P // pieces[name]
+            src = raw[name, h][:].rearrange("p j (m u e) -> p u m j e", u=2, e=2)
+            dst = staged[name, u][:].rearrange("p e m j -> p m j e")
+            copy(out=dst[:, h * width : (h + 1) * width, :, :], in_=src[:, u, :, :, :])
 
         def quantise(name, u):
             nc.vector.quantize_mx(
@@ -123,24 +117,27 @@ def tile_picked_zwave_glu_po_kernel(
 
         def multiply_half(acc, name, d, u, h):
             for e in range(2):
+                alone = acc is f_acc and (h, u) == (0, 0)
                 multiply(
-                    acc[h][u][:, e, :], name, d, u, e, slice(h * HALF, (h + 1) * HALF),
-                    d == 0 and e == 0, d == TAPS - 1 and e == 1,
+                    acc[h][u][e], name, d, u, e, slice(h * HALF, (h + 1) * HALF),
+                    d == 0 and (e == 0 or alone), d == TAPS - 1 and (e == 1 or alone),
                 )
 
         def multiply_all(acc, name, d, u):
             for h in range(2):
                 multiply_half(acc, name, d, u, h)
 
-        def gates(h, tag):
-            gate = keep.tile([P, PACK, HALF], F32, name=f"gate{h}", tag=tag, align_bytes=64)
-            for u in range(2):
-                nc.scalar.activation(gate[:, 2 * u : 2 * u + 2, :], g_acc[h][u][:], SIGMOID)
-            return gate
+        def gates(banks, tag):
+            tile = keep.tile([P, len(banks), 2, HALF], F32, name=f"gate_after_{tag}", tag=tag, align_bytes=64)
+            for i, (h, u) in enumerate(banks):
+                nc.scalar.activation(tile[:, i, :, :], g_bank[h][u][:], SIGMOID)
+                gate[h, u] = tile[:, i, :, :]
 
         on_s, on_v = nc.scalar.copy, nc.vector.tensor_copy
-        g_acc = [[psum.tile([P, 2, HALF], F32, name=f"g_acc{h}_{u}") for u in range(2)] for h in range(2)]
-        f_acc = [[psum.tile([P, 2, HALF], F32, name=f"f_acc{h}_{u}") for u in range(2)] for h in range(2)]
+        g_bank = [[psum.tile([P, 2, HALF], F32, name=f"g_bank{h}_{u}", tag=f"g_bank{h}_{u}") for u in range(2)] for h in range(2)]
+        f_bank = [[psum.tile([P, 2, HALF], F32, name=f"f_bank{h}_{u}") for u in range(2)] for h in range(2)]
+        g_acc = [[[g_bank[h][u][:, e, :] for e in range(2)] for u in range(2)] for h in range(2)]
+        f_acc = [[[f_bank[h][u][:, e, :] for e in range(2)] for u in range(2)] for h in range(2)]
 
         for d in range(TAPS):
             name = f"v{d}"
@@ -151,23 +148,28 @@ def tile_picked_zwave_glu_po_kernel(
                 multiply_all(g_acc, name, d, u)
                 if d == 0:
                     gather_words(u + 1, f"staged_v0_{u}")
-        gate = []
-        for d in range(TAPS - 1):
-            name = f"w{d}"
-            cast(on_v, name, 1)
-            cast(on_s, name, 0)
-            for u in (1, 0):
-                quantise(name, u)
-                multiply_all(f_acc, name, d, u)
-            if d == 0:
-                gate.append(gates(0, "raw_w0"))
+        cast(on_v, "w0", 1)
+        cast(on_s, "w0", 0)
+        gate = {}
+        gates([(0, 0)], "raw_w0_0")
+        f_second = psum.tile([P, HALF], F32, name="f_second", tag="g_bank0_0")
+        f_acc[0][0][1] = f_second[:]
+        for u in (1, 0):
+            quantise("w0", u)
+            multiply_all(f_acc, "w0", 0, u)
         for h in range(2):
-            cast_last(on_v, h, 0)
-            cast_last(on_s, h, 1)
+            cast(on_v, "w1", 1, h)
+            cast(on_s, "w1", 0, h)
+        for u in (1, 0):
+            quantise("w1", u)
+            multiply_all(f_acc, "w1", 1, u)
+        for h in range(2):
+            cast(on_v, "w2", 0, h)
+            cast(on_s, "w2", 1, h)
             for u in range(2):
                 for e in range(2):
                     quantise_last(h, u, e)
-        gate.append(gates(1, "raw_w2_1"))
+        gates([(0, 1), (1, 0), (1, 1)], "raw_w2_1")
         for h in range(2):
             for u in range(2):
                 multiply_half(f_acc, "w2", TAPS - 1, u, h)
@@ -179,12 +181,11 @@ def tile_picked_zwave_glu_po_kernel(
         ys = [keep.tile([P, PACK, HALF], F32, name=f"y{h}", align_bytes=64) for h in range(2)]
         rounded = [keep.tile([P, QUARTER, PACK], BF16, name=f"rounded{c}", align_bytes=64) for c in range(4)]
 
-        def gate_half(h):
-            cols = slice(h * HALF, (h + 1) * HALF)
-            for u in range(2):
-                pair = slice(2 * u, 2 * u + 2)
-                nc.vector.tensor_tensor(ys[h][:, pair, :], f_acc[h][u][:], gate[h][:, pair, :], MULT)
-                nc.sync.dma_start(out=out_rows[:, pair, cols], in_=ys[h][:, pair, :])
+        def store(h, tiles):
+            nc.sync.dma_start(out=out_rows[:, tiles, h * HALF : (h + 1) * HALF], in_=ys[h][:, tiles, :])
+
+        def gate_pair(h, u):
+            nc.vector.tensor_tensor(ys[h][:, 2 * u : 2 * u + 2, :], f_bank[h][u][:], gate[h, u], MULT)
 
         def round_quarter(copy, c):
             h, part = divmod(c, 2)
@@ -202,18 +203,24 @@ def tile_picked_zwave_glu_po_kernel(
                 in_=rounded[c][:].rearrange("p c t -> p (c t)"),
             )
 
-        gate_half(0)
+        for e in range(2):
+            nc.vector.tensor_tensor(ys[0][:, e, :], f_acc[0][0][e], gate[0, 0][:, e, :], MULT)
+        store(0, slice(0, 2))
+        gate_pair(0, 1)
+        store(0, slice(2, 4))
         round_quarter(on_s, 0)
         round_quarter(on_s, 1)
-        gate_half(1)
-        round_quarter(on_s, 2)
+        for u in range(2):
+            gate_pair(1, u)
+            store(1, slice(2 * u, 2 * u + 2))
+        round_quarter(on_s, 3)
         finish(0)
-        round_quarter(on_v, 3)
+        round_quarter(on_v, 2)
         finish(1)
-        nc.sync.dma_start(out=out_words[:, 0:HALF], in_=y_codes[:, 0:HALF].bitcast(I32))
-        finish(3)
         finish(2)
-        nc.sync.dma_start(out=out_words[:, HALF:S], in_=y_codes[:, HALF:S].bitcast(I32))
+        nc.sync.dma_start(out=out_words[:, : 3 * QUARTER], in_=y_codes[:, : 3 * QUARTER].bitcast(I32))
+        finish(3)
+        nc.sync.dma_start(out=out_words[:, 3 * QUARTER :], in_=y_codes[:, 3 * QUARTER :].bitcast(I32))
         for q in range(4):
             queue = nc.sync if q % 2 == 0 else nc.scalar
             queue.dma_start(

@@ -44,7 +44,7 @@ def tile_picked_zwave_glu_po_kernel(
             )
 
         names = ("v0", "v1", "v2", "w0", "w1", "w2")
-        pieces = {"v0": 1, "v1": 1, "v2": 1, "w0": 1, "w1": 2, "w2": 2}
+        pieces = {"v0": 1, "v1": 1, "v2": 1, "w0": 1, "w1": 1, "w2": 2}
         raw = {}
         for name, src in zip(names, (v0, v1, v2, w0, w1, w2)):
             width = N // pieces[name]
@@ -157,9 +157,8 @@ def tile_picked_zwave_glu_po_kernel(
         for u in (1, 0):
             quantise("w0", u)
             multiply_all(f_acc, "w0", 0, u)
-        for h in range(2):
-            cast(on_v, "w1", 1, h)
-            cast(on_s, "w1", 0, h)
+        cast(on_v, "w1", 1)
+        cast(on_s, "w1", 0)
         for u in (1, 0):
             quantise("w1", u)
             multiply_all(f_acc, "w1", 1, u)

@@ -29,9 +29,9 @@ def tile_picked_zwave_glu_po_kernel(
         keep = ctx.enter_context(tc.tile_pool(name="keep", bufs=1))
         psum = ctx.enter_context(tc.psum_pool(name="psum", bufs=1))
 
-        lists = [keep.tile([P, S // 16], U16, name=f"list{d}") for d in range(TAPS)]
-        table_words = keep.tile([P, T], U32, name="table_words", align_bytes=64)
-        table_scales = keep.tile([P, T], U8, name="table_scales", align_bytes=64)
+        lists = [keep.tile([P, S // 16], U16, name=f"list{d}", align_bytes=256) for d in range(TAPS)]
+        table_words = keep.tile([P, T], U32, name="table_words", align_bytes=256)
+        table_scales = keep.tile([P, T], U8, name="table_scales", align_bytes=256)
         words_in = x_words[0].rearrange("p c r -> p (c r)").bitcast(I32)
         nc.vector.memset(table_scales[:].bitcast(I32), 0)
         nc.sync.dma_start(out=table_words[:, : T // 2].bitcast(I32), in_=words_in[:, : T // 2])
@@ -49,7 +49,7 @@ def tile_picked_zwave_glu_po_kernel(
         for name, src in zip(names, (v0, v1, v2, w0, w1, w2)):
             width = N // pieces[name]
             for h in range(pieces[name]):
-                raw[name, h] = keep.tile([P, PACK, width], F32, name=f"raw_{name}_{h}", tag=f"raw_{name}_{h}", align_bytes=64)
+                raw[name, h] = keep.tile([P, PACK, width], F32, name=f"raw_{name}_{h}", tag=f"raw_{name}_{h}", align_bytes=256)
                 nc.sync.dma_start(
                     out=raw[name, h][:], in_=src.rearrange("(p j) c -> p j c", j=PACK)[:, :, h * width : (h + 1) * width]
                 )
@@ -64,12 +64,12 @@ def tile_picked_zwave_glu_po_kernel(
 
         picked_words, picked_scales = [], []
         for d in range(TAPS):
-            ps = keep.tile([P, S], U8, name=f"picked_scales{d}", align_bytes=64)
+            ps = keep.tile([P, S], U8, name=f"picked_scales{d}", align_bytes=256)
             nc.vector.tensor_copy(ps[:], table_scales[:].indirect(lists[d][:]))
             picked_scales.append(ps)
 
         def gather_words(d, tag):
-            pw = keep.tile([P, S], U32, name=f"picked_words{d}", tag=tag, align_bytes=64)
+            pw = keep.tile([P, S], U32, name=f"picked_words{d}", tag=tag, align_bytes=256)
             nc.vector.tensor_copy(pw[:], table_words[:].indirect(lists[d][:]))
             picked_words.append(pw)
 
@@ -78,9 +78,9 @@ def tile_picked_zwave_glu_po_kernel(
         staged, codes, scales = {}, {}, {}
         for name in names:
             for u in range(2):
-                staged[name, u] = keep.tile([P, 2, P, PACK], BF16, name=f"staged_{name}_{u}", tag=f"staged_{name}_{u}", align_bytes=64)
-                codes[name, u] = keep.tile([P, 2 * P], U32, name=f"codes_{name}_{u}", align_bytes=64)
-                scales[name, u] = keep.tile([P, 2 * P], U8, name=f"scales_{name}_{u}", align_bytes=64)
+                staged[name, u] = keep.tile([P, 2, P, PACK], BF16, name=f"staged_{name}_{u}", tag=f"staged_{name}_{u}", align_bytes=256)
+                codes[name, u] = keep.tile([P, 2 * P], U32, name=f"codes_{name}_{u}", align_bytes=256)
+                scales[name, u] = keep.tile([P, 2 * P], U8, name=f"scales_{name}_{u}", align_bytes=256)
 
         def cast(copy, name, u, h=0):
             width = P // pieces[name]
@@ -128,7 +128,7 @@ def tile_picked_zwave_glu_po_kernel(
                 multiply_half(acc, name, d, u, h)
 
         def gates(banks, tag):
-            tile = keep.tile([P, len(banks), 2, HALF], F32, name=f"gate_after_{tag}", tag=tag, align_bytes=64)
+            tile = keep.tile([P, len(banks), 2, HALF], F32, name=f"gate_after_{tag}", tag=tag, align_bytes=256)
             for i, (h, u) in enumerate(banks):
                 nc.scalar.activation(tile[:, i, :, :], g_bank[h][u][:], SIGMOID)
                 gate[h, u] = tile[:, i, :, :]
@@ -173,12 +173,12 @@ def tile_picked_zwave_glu_po_kernel(
             for u in range(2):
                 multiply_half(f_acc, "w2", TAPS - 1, u, h)
 
-        y_codes = keep.tile([P, S], U32, name="y_codes", align_bytes=64)
-        y_scales = keep.tile([P, S], U8, name="y_scales", align_bytes=64)
+        y_codes = keep.tile([P, S], U32, name="y_codes", align_bytes=256)
+        y_scales = keep.tile([P, S], U8, name="y_scales", align_bytes=256)
         out_rows = out_0.rearrange("(p t) j -> p t j", t=PACK)
         out_words = out_1[0].rearrange("p c r -> p (c r)").bitcast(I32)
-        ys = [keep.tile([P, PACK, HALF], F32, name=f"y{h}", align_bytes=64) for h in range(2)]
-        rounded = [keep.tile([P, QUARTER, PACK], BF16, name=f"rounded{c}", align_bytes=64) for c in range(4)]
+        ys = [keep.tile([P, PACK, HALF], F32, name=f"y{h}", align_bytes=256) for h in range(2)]
+        rounded = [keep.tile([P, QUARTER, PACK], BF16, name=f"rounded{c}", align_bytes=256) for c in range(4)]
 
         def store(h, tiles):
             nc.sync.dma_start(out=out_rows[:, tiles, h * HALF : (h + 1) * HALF], in_=ys[h][:, tiles, :])

@@ -190,8 +190,8 @@ def tile_picked_zwave_glu_po_kernel(
             h, part = divmod(c, 2)
             src = ys[h][:, :, part * QUARTER : (part + 1) * QUARTER]
             copy(
-                out=rounded[c][:].rearrange("p (c i) t -> p c t i", i=2),
-                in_=src.rearrange("p t (c i) -> p c t i", i=2),
+                out=rounded[c][:].rearrange("p (c i) t -> p c t i", i=4),
+                in_=src.rearrange("p t (c i) -> p c t i", i=4),
             )
 
         def finish(c):
@@ -214,12 +214,12 @@ def tile_picked_zwave_glu_po_kernel(
             store(1, slice(2 * u, 2 * u + 2))
         round_quarter(on_s, 3)
         finish(0)
-        round_quarter(on_v, 2)
         finish(1)
-        finish(2)
-        nc.sync.dma_start(out=out_words[:, : 3 * QUARTER], in_=y_codes[:, : 3 * QUARTER].bitcast(I32))
+        nc.sync.dma_start(out=out_words[:, :HALF], in_=y_codes[:, :HALF].bitcast(I32))
+        round_quarter(on_v, 2)
         finish(3)
-        nc.sync.dma_start(out=out_words[:, 3 * QUARTER :], in_=y_codes[:, 3 * QUARTER :].bitcast(I32))
+        finish(2)
+        nc.sync.dma_start(out=out_words[:, HALF:], in_=y_codes[:, HALF:].bitcast(I32))
         for q in range(4):
             queue = nc.sync if q % 2 == 0 else nc.scalar
             queue.dma_start(

@@ -19,6 +19,9 @@ MULT = mybir.AluOpType.mult
 P = 128
 PACK = 4
 HALF, QUARTER = S // 2, S // 4
+ON_VECTOR = 192
+W1_SPLIT = 84
+LAST_SPLITS = (32, 40)
 
 
 def tile_picked_zwave_glu_po_kernel(
@@ -73,42 +76,38 @@ def tile_picked_zwave_glu_po_kernel(
             nc.vector.tensor_copy(pw[:], table_words[:].indirect(lists[d][:]))
             picked_words.append(pw)
 
-        gather_words(0, "picked_words0")
+        for d in range(2):
+            gather_words(d, f"picked_words{d}")
 
         staged, codes, scales = {}, {}, {}
         for name in names:
-            for u in range(2):
-                staged[name, u] = keep.tile([P, 2, P, PACK], BF16, name=f"staged_{name}_{u}", tag=f"staged_{name}_{u}", align_bytes=256)
-                codes[name, u] = keep.tile([P, 2 * P], U32, name=f"codes_{name}_{u}", align_bytes=256)
-                scales[name, u] = keep.tile([P, 2 * P], U8, name=f"scales_{name}_{u}", align_bytes=256)
+            staged[name] = keep.tile([P, PACK, P, PACK], BF16, name=f"staged_{name}", tag=f"staged_{name}", align_bytes=256)
+            codes[name] = keep.tile([P, N], U32, name=f"codes_{name}", align_bytes=256)
+            scales[name] = keep.tile([P, N], U8, name=f"scales_{name}", align_bytes=256)
 
-        def cast(copy, name, u, h=0):
-            width = P // pieces[name]
-            src = raw[name, h][:].rearrange("p j (m u e) -> p u m j e", u=2, e=2)
-            dst = staged[name, u][:].rearrange("p e m j -> p m j e")
-            copy(out=dst[:, h * width : (h + 1) * width, :, :], in_=src[:, u, :, :, :])
+        def cast(copy, name, h, first, last):
+            offset = h * (P // pieces[name])
+            src = raw[name, h][:].rearrange("p j (m i t) -> p m j i t", i=2, t=PACK)
+            dst = staged[name][:].rearrange("p t (m i) j -> p m j i t", i=2)
+            copy(out=dst[:, (offset + first) // 2 : (offset + last) // 2], in_=src[:, first // 2 : last // 2])
 
-        def quantise(name, u):
+        def cast_shared(name, h, split):
+            cast(on_v, name, h, 0, split)
+            cast(on_s, name, h, split, P // pieces[name])
+
+        def quantise(name, first, last):
             nc.vector.quantize_mx(
-                out=codes[name, u][:].bitcast(FP8X4),
-                scales=scales[name, u][:],
-                in_=staged[name, u][:].rearrange("p e m j -> p (e m j)"),
-            )
-
-        def quantise_last(h, u, e):
-            cols = slice(e * P + h * (P // 2), e * P + (h + 1) * (P // 2))
-            nc.vector.quantize_mx(
-                out=codes["w2", u][:, cols].bitcast(FP8X4),
-                scales=scales["w2", u][:, cols],
-                in_=staged["w2", u][:, e, h * (P // 2) : (h + 1) * (P // 2), :].rearrange("p m j -> p (m j)"),
+                out=codes[name][:, first:last].bitcast(FP8X4),
+                scales=scales[name][:, first:last],
+                in_=staged[name][:].rearrange("p t m j -> p (t m j)")[:, PACK * first : PACK * last],
             )
 
         def multiply(out, name, d, u, e, frames, start, stop):
-            cols = slice(e * P, (e + 1) * P)
+            cols = slice((2 * u + e) * P, (2 * u + e + 1) * P)
             nc.tensor.matmul_mx(
                 out=out,
-                lhsT=codes[name, u][:, cols].bitcast(FP8X4),
-                lhsT_scale=scales[name, u][:, cols],
+                lhsT=codes[name][:, cols].bitcast(FP8X4),
+                lhsT_scale=scales[name][:, cols],
                 rhs=picked_words[d][:, frames].bitcast(FP8X4),
                 rhs_scale=picked_scales[d][:, frames],
                 start=start,
@@ -123,9 +122,10 @@ def tile_picked_zwave_glu_po_kernel(
                     d == 0 and (e == 0 or alone), d == TAPS - 1 and (e == 1 or alone),
                 )
 
-        def multiply_all(acc, name, d, u):
+        def multiply_all(acc, name, d):
             for h in range(2):
-                multiply_half(acc, name, d, u, h)
+                for u in range(2):
+                    multiply_half(acc, name, d, u, h)
 
         def gates(banks, tag):
             tile = keep.tile([P, len(banks), 2, HALF], F32, name=f"gate_after_{tag}", tag=tag, align_bytes=256)
@@ -141,85 +141,79 @@ def tile_picked_zwave_glu_po_kernel(
 
         for d in range(TAPS):
             name = f"v{d}"
-            cast(on_s, name, 0)
-            cast(on_v if d == TAPS - 1 else on_s, name, 1)
-            for u in range(2):
-                quantise(name, u)
-                multiply_all(g_acc, name, d, u)
-                if d == 0:
-                    gather_words(u + 1, f"staged_v0_{u}")
-        cast(on_v, "w0", 1)
-        cast(on_s, "w0", 0)
+            if d < TAPS - 1:
+                cast(on_s, name, 0, 0, P)
+            else:
+                cast_shared(name, 0, P // 2)
+            quantise(name, 0, N)
+            multiply_all(g_acc, name, d)
+            if d == 0:
+                gather_words(2, "staged_v0")
+        cast_shared("w0", 0, P // 2)
         gate = {}
         gates([(0, 0)], "raw_w0_0")
         f_second = psum.tile([P, HALF], F32, name="f_second", tag="g_bank0_0")
         f_acc[0][0][1] = f_second[:]
-        for u in (1, 0):
-            quantise("w0", u)
-            multiply_all(f_acc, "w0", 0, u)
-        cast(on_v, "w1", 1)
-        cast(on_s, "w1", 0)
-        for u in (1, 0):
-            quantise("w1", u)
-            multiply_all(f_acc, "w1", 1, u)
-        for h in range(2):
-            cast(on_v, "w2", 0, h)
-            cast(on_s, "w2", 1, h)
-            for u in range(2):
-                for e in range(2):
-                    quantise_last(h, u, e)
+        quantise("w0", 0, N)
+        multiply_all(f_acc, "w0", 0)
+        cast_shared("w1", 0, W1_SPLIT)
+        quantise("w1", 0, N)
+        multiply_all(f_acc, "w1", 1)
+        for h, split in enumerate(LAST_SPLITS):
+            cast_shared("w2", h, split)
+        for first, last in ((0, P), (P, 2 * P), (2 * P, N)):
+            quantise("w2", first, last)
         gates([(0, 1), (1, 0), (1, 1)], "raw_w2_1")
-        for h in range(2):
-            for u in range(2):
-                multiply_half(f_acc, "w2", TAPS - 1, u, h)
+        multiply_all(f_acc, "w2", TAPS - 1)
 
         y_codes = keep.tile([P, S], U32, name="y_codes", align_bytes=256)
         y_scales = keep.tile([P, S], U8, name="y_scales", align_bytes=256)
         out_rows = out_0.rearrange("(p t) j -> p t j", t=PACK)
         out_words = out_1[0].rearrange("p c r -> p (c r)").bitcast(I32)
         ys = [keep.tile([P, PACK, HALF], F32, name=f"y{h}", align_bytes=256) for h in range(2)]
-        rounded = [keep.tile([P, QUARTER, PACK], BF16, name=f"rounded{c}", align_bytes=256) for c in range(4)]
+        rounded = [keep.tile([P, HALF, PACK], BF16, name=f"rounded{h}", align_bytes=256) for h in range(2)]
 
         def store(h, tiles):
             nc.sync.dma_start(out=out_rows[:, tiles, h * HALF : (h + 1) * HALF], in_=ys[h][:, tiles, :])
 
-        def gate_pair(h, u):
-            nc.vector.tensor_tensor(ys[h][:, 2 * u : 2 * u + 2, :], f_bank[h][u][:], gate[h, u], MULT)
-
-        def round_quarter(copy, c):
-            h, part = divmod(c, 2)
-            src = ys[h][:, :, part * QUARTER : (part + 1) * QUARTER]
-            copy(
-                out=rounded[c][:].rearrange("p (c i) t -> p c t i", i=4),
-                in_=src.rearrange("p t (c i) -> p c t i", i=4),
+        def gate_pair(h, u, first, last):
+            nc.vector.tensor_tensor(
+                ys[h][:, 2 * u : 2 * u + 2, first:last], f_bank[h][u][:, :, first:last], gate[h, u][:, :, first:last], MULT
             )
 
-        def finish(c):
-            cols = slice(c * QUARTER, (c + 1) * QUARTER)
+        def round_frames(copy, h, first, last):
+            copy(
+                out=rounded[h][:, first:last, :].rearrange("p (c i) t -> p c t i", i=4),
+                in_=ys[h][:, :, first:last].rearrange("p t (c i) -> p c t i", i=4),
+            )
+
+        def finish(h, first, last):
+            cols = slice(h * HALF + first, h * HALF + last)
             nc.vector.quantize_mx(
                 out=y_codes[:, cols].bitcast(FP8X4),
                 scales=y_scales[:, cols],
-                in_=rounded[c][:].rearrange("p c t -> p (c t)"),
+                in_=rounded[h][:, first:last, :].rearrange("p c t -> p (c t)"),
             )
 
         for e in range(2):
             nc.vector.tensor_tensor(ys[0][:, e, :], f_acc[0][0][e], gate[0, 0][:, e, :], MULT)
         store(0, slice(0, 2))
-        gate_pair(0, 1)
+        gate_pair(0, 1, 0, HALF)
         store(0, slice(2, 4))
-        round_quarter(on_s, 0)
-        round_quarter(on_s, 1)
-        for u in range(2):
-            gate_pair(1, u)
-            store(1, slice(2 * u, 2 * u + 2))
-        round_quarter(on_s, 3)
-        finish(0)
-        finish(1)
-        nc.sync.dma_start(out=out_words[:, :HALF], in_=y_codes[:, :HALF].bitcast(I32))
-        round_quarter(on_v, 2)
-        finish(3)
-        finish(2)
-        nc.sync.dma_start(out=out_words[:, HALF:], in_=y_codes[:, HALF:].bitcast(I32))
+        round_frames(on_s, 0, 0, QUARTER)
+        round_frames(on_s, 0, QUARTER, HALF)
+        gate_pair(1, 0, 0, HALF)
+        store(1, slice(0, 2))
+        gate_pair(1, 1, 0, QUARTER)
+        gate_pair(1, 1, QUARTER, HALF)
+        store(1, slice(2, 4))
+        round_frames(on_v, 1, 0, QUARTER)
+        round_frames(on_v, 1, QUARTER, ON_VECTOR)
+        round_frames(on_s, 1, ON_VECTOR, HALF)
+        for h in range(2):
+            finish(h, 0, HALF)
+            cols = slice(h * HALF, (h + 1) * HALF)
+            nc.sync.dma_start(out=out_words[:, cols], in_=y_codes[:, cols].bitcast(I32))
         for q in range(4):
             queue = nc.sync if q % 2 == 0 else nc.scalar
             queue.dma_start(

@@ -20,8 +20,8 @@ P = 128
 PACK = 4
 HALF, QUARTER = S // 2, S // 4
 ON_VECTOR = 192
-W1_SPLIT = 84
-LAST_SPLITS = (32, 40)
+V2_SPLIT = 32
+FIRST = T // 2
 
 
 def tile_picked_zwave_glu_po_kernel(
@@ -37,7 +37,7 @@ def tile_picked_zwave_glu_po_kernel(
         table_scales = keep.tile([P, T], U8, name="table_scales", align_bytes=256)
         words_in = x_words[0].rearrange("p c r -> p (c r)").bitcast(I32)
         nc.vector.memset(table_scales[:].bitcast(I32), 0)
-        nc.sync.dma_start(out=table_words[:, : T // 2].bitcast(I32), in_=words_in[:, : T // 2])
+        nc.sync.dma_start(out=table_words[:, :FIRST].bitcast(I32), in_=words_in[:, :FIRST])
         nc.sync.dma_start(lists[0][:], offs)
         nc.sync.dma_start(lists[1][:], back1)
         for r in range(4):
@@ -58,7 +58,7 @@ def tile_picked_zwave_glu_po_kernel(
                 )
             if name == "v0":
                 nc.sync.dma_start(lists[2][:], back2)
-                nc.sync.dma_start(out=table_words[:, T // 2 :].bitcast(I32), in_=words_in[:, T // 2 :])
+                nc.sync.dma_start(out=table_words[:, FIRST:].bitcast(I32), in_=words_in[:, FIRST:])
 
         warm_in = keep.tile([P, 1], F32, name="warm_in")
         warm_out = keep.tile([P, 1], F32, name="warm_out")
@@ -85,15 +85,19 @@ def tile_picked_zwave_glu_po_kernel(
             codes[name] = keep.tile([P, N], U32, name=f"codes_{name}", align_bytes=256)
             scales[name] = keep.tile([P, N], U8, name=f"scales_{name}", align_bytes=256)
 
-        def cast(copy, name, h, first, last):
-            offset = h * (P // pieces[name])
-            src = raw[name, h][:].rearrange("p j (m i t) -> p m j i t", i=2, t=PACK)
+        def cast(copy, name, first, last):
+            src = raw[name, 0][:].rearrange("p j (m i t) -> p m j i t", i=2, t=PACK)
             dst = staged[name][:].rearrange("p t (m i) j -> p m j i t", i=2)
-            copy(out=dst[:, (offset + first) // 2 : (offset + last) // 2], in_=src[:, first // 2 : last // 2])
+            copy(out=dst[:, first // 2 : last // 2], in_=src[:, first // 2 : last // 2])
 
-        def cast_shared(name, h, split):
-            cast(on_v, name, h, 0, split)
-            cast(on_s, name, h, split, P // pieces[name])
+        def cast_shared(name, split):
+            cast(on_v, name, 0, split)
+            cast(on_s, name, split, P)
+
+        def cast_pair(copy, name, h, u):
+            src = raw[name, h][:].rearrange("p j (m u e) -> p u m j e", u=2, e=2)
+            dst = staged[name][:].rearrange("p (u e) (h m) j -> p h u m j e", u=2, h=pieces[name])
+            copy(out=dst[:, h, u], in_=src[:, u])
 
         def quantise(name, first, last):
             nc.vector.quantize_mx(
@@ -122,9 +126,9 @@ def tile_picked_zwave_glu_po_kernel(
                     d == 0 and (e == 0 or alone), d == TAPS - 1 and (e == 1 or alone),
                 )
 
-        def multiply_all(acc, name, d):
+        def multiply_all(acc, name, d, pairs=(0, 1)):
             for h in range(2):
-                for u in range(2):
+                for u in pairs:
                     multiply_half(acc, name, d, u, h)
 
         def gates(banks, tag):
@@ -142,27 +146,30 @@ def tile_picked_zwave_glu_po_kernel(
         for d in range(TAPS):
             name = f"v{d}"
             if d < TAPS - 1:
-                cast(on_s, name, 0, 0, P)
+                cast(on_s, name, 0, P)
             else:
-                cast_shared(name, 0, P // 2)
+                cast_shared(name, V2_SPLIT)
             quantise(name, 0, N)
             multiply_all(g_acc, name, d)
             if d == 0:
                 gather_words(2, "staged_v0")
-        cast_shared("w0", 0, P // 2)
+        cast_shared("w0", P // 2)
         gate = {}
         gates([(0, 0)], "raw_w0_0")
         f_second = psum.tile([P, HALF], F32, name="f_second", tag="g_bank0_0")
         f_acc[0][0][1] = f_second[:]
         quantise("w0", 0, N)
         multiply_all(f_acc, "w0", 0)
-        cast_shared("w1", 0, W1_SPLIT)
-        quantise("w1", 0, N)
-        multiply_all(f_acc, "w1", 1)
-        for h, split in enumerate(LAST_SPLITS):
-            cast_shared("w2", h, split)
-        for first, last in ((0, P), (P, 2 * P), (2 * P, N)):
-            quantise("w2", first, last)
+        cast_pair(on_v, "w1", 0, 1)
+        cast_pair(on_s, "w1", 0, 0)
+        for u in (1, 0):
+            quantise("w1", 2 * u * P, 2 * (u + 1) * P)
+            multiply_all(f_acc, "w1", 1, (u,))
+        for h in range(2):
+            cast_pair(on_v, "w2", h, 0)
+            cast_pair(on_s, "w2", h, 1)
+            for t in range(PACK):
+                quantise("w2", t * P + h * (P // 2), t * P + (h + 1) * (P // 2))
         gates([(0, 1), (1, 0), (1, 1)], "raw_w2_1")
         multiply_all(f_acc, "w2", TAPS - 1)
 
@@ -198,7 +205,8 @@ def tile_picked_zwave_glu_po_kernel(
         for e in range(2):
             nc.vector.tensor_tensor(ys[0][:, e, :], f_acc[0][0][e], gate[0, 0][:, e, :], MULT)
         store(0, slice(0, 2))
-        gate_pair(0, 1, 0, HALF)
+        gate_pair(0, 1, 0, QUARTER)
+        gate_pair(0, 1, QUARTER, HALF)
         store(0, slice(2, 4))
         round_frames(on_s, 0, 0, QUARTER)
         round_frames(on_s, 0, QUARTER, HALF)

@@ -166,10 +166,12 @@ def tile_picked_zwave_glu_po_kernel(
             quantise("w1", 2 * u * P, 2 * (u + 1) * P)
             multiply_all(f_acc, "w1", 1, (u,))
         for h in range(2):
-            cast_pair(on_v, "w2", h, 0)
-            cast_pair(on_s, "w2", h, 1)
-            for t in range(PACK):
+            cast_pair(on_v, "w2", h, 1 - h)
+            cast_pair(on_s, "w2", h, h)
+            for t in range(2):
                 quantise("w2", t * P + h * (P // 2), t * P + (h + 1) * (P // 2))
+        for t in range(2, PACK):
+            quantise("w2", t * P, (t + 1) * P)
         gates([(0, 1), (1, 0), (1, 1)], "raw_w2_1")
         multiply_all(f_acc, "w2", TAPS - 1)
 

@@ -21,6 +21,8 @@ PACK = 4
 HALF, QUARTER = S // 2, S // 4
 ON_VECTOR = 192
 V2_SPLIT = 32
+W1_EXTRA = 32
+LAST_EXTRA = 16
 FIRST = T // 2
 
 
@@ -94,10 +96,10 @@ def tile_picked_zwave_glu_po_kernel(
             cast(on_v, name, 0, split)
             cast(on_s, name, split, P)
 
-        def cast_pair(copy, name, h, u):
+        def cast_pair(copy, name, h, u, columns=slice(None)):
             src = raw[name, h][:].rearrange("p j (m u e) -> p u m j e", u=2, e=2)
             dst = staged[name][:].rearrange("p (u e) (h m) j -> p h u m j e", u=2, h=pieces[name])
-            copy(out=dst[:, h, u], in_=src[:, u])
+            copy(out=dst[:, h, u, columns], in_=src[:, u, columns])
 
         def quantise(name, first, last):
             nc.vector.quantize_mx(
@@ -161,17 +163,22 @@ def tile_picked_zwave_glu_po_kernel(
         quantise("w0", 0, N)
         multiply_all(f_acc, "w0", 0)
         cast_pair(on_v, "w1", 0, 1)
-        cast_pair(on_s, "w1", 0, 0)
+        cast_pair(on_v, "w1", 0, 0, slice(0, W1_EXTRA))
+        cast_pair(on_s, "w1", 0, 0, slice(W1_EXTRA, P))
         for u in (1, 0):
             quantise("w1", 2 * u * P, 2 * (u + 1) * P)
             multiply_all(f_acc, "w1", 1, (u,))
-        for h in range(2):
-            cast_pair(on_v, "w2", h, 1 - h)
-            cast_pair(on_s, "w2", h, h)
-            for t in range(2):
-                quantise("w2", t * P + h * (P // 2), t * P + (h + 1) * (P // 2))
+        for u in range(2):
+            cast_pair(on_s, "w2", 0, u)
+        for t in range(2):
+            quantise("w2", t * P, t * P + P // 2)
+        cast_pair(on_v, "w2", 1, 0)
+        cast_pair(on_v, "w2", 1, 1, slice(0, LAST_EXTRA))
+        cast_pair(on_s, "w2", 1, 1, slice(LAST_EXTRA, P // 2))
         for t in range(2, PACK):
-            quantise("w2", t * P, (t + 1) * P)
+            quantise("w2", t * P, t * P + P // 2)
+        for t in range(PACK):
+            quantise("w2", t * P + P // 2, (t + 1) * P)
         gates([(0, 1), (1, 0), (1, 1)], "raw_w2_1")
         multiply_all(f_acc, "w2", TAPS - 1)
 

from contextlib import ExitStack

import concourse.mybir as mybir

K, T, S, N = 512, 2048, 512, 512
TAPS = 3
FLOPS = 2 * TAPS * 2 * K * N * S

F32 = mybir.dt.float32
BF16 = mybir.dt.bfloat16
I32 = mybir.dt.int32
U32 = mybir.dt.uint32
U16 = mybir.dt.uint16
U8 = mybir.dt.uint8
FP8X4 = mybir.dt.float8_e4m3fn_x4
SIGMOID = mybir.ActivationFunctionType.Sigmoid
MULT = mybir.AluOpType.mult

P = 128
PACK = 4
HALF, QUARTER = S // 2, S // 4
ON_VECTOR = 192
V2_SPLIT = 32
W1_EXTRA = 32
LAST_EXTRA = 16
FIRST = T // 2


def tile_picked_zwave_glu_po_kernel(
    tc, x_words, x_scales, w0, v0, w1, v1, w2, v2, offs, back1, back2, out_0, out_1, out_2
):
    nc = tc.nc
    with ExitStack() as ctx:
        keep = ctx.enter_context(tc.tile_pool(name="keep", bufs=1))
        psum = ctx.enter_context(tc.psum_pool(name="psum", bufs=1))

        lists = [keep.tile([P, S // 16], U16, name=f"list{d}", align_bytes=256) for d in range(TAPS)]
        table_words = keep.tile([P, T], U32, name="table_words", align_bytes=256)
        table_scales = keep.tile([P, T], U8, name="table_scales", align_bytes=256)
        words_in = x_words[0].rearrange("p c r -> p (c r)").bitcast(I32)
        nc.vector.memset(table_scales[:].bitcast(I32), 0)
        nc.sync.dma_start(out=table_words[:, :FIRST].bitcast(I32), in_=words_in[:, :FIRST])
        nc.sync.dma_start(lists[0][:], offs)
        nc.sync.dma_start(lists[1][:], back1)
        for r in range(4):
            nc.sync.dma_start(
                out=table_scales[r:P:32, :].bitcast(I32),
                in_=x_scales[0, r:16:4, :].bitcast(I32),
            )

        names = ("v0", "v1", "v2", "w0", "w1", "w2")
        pieces = {"v0": 1, "v1": 1, "v2": 1, "w0": 1, "w1": 1, "w2": 2}
        raw = {}
        for name, src in zip(names, (v0, v1, v2, w0, w1, w2)):
            width = N // pieces[name]
            for h in range(pieces[name]):
                raw[name, h] = keep.tile([P, PACK, width], F32, name=f"raw_{name}_{h}", tag=f"raw_{name}_{h}", align_bytes=256)
                nc.sync.dma_start(
                    out=raw[name, h][:], in_=src.rearrange("(p j) c -> p j c", j=PACK)[:, :, h * width : (h + 1) * width]
                )
            if name == "v0":
                nc.sync.dma_start(lists[2][:], back2)
                nc.sync.dma_start(out=table_words[:, FIRST:].bitcast(I32), in_=words_in[:, FIRST:])

        warm_in = keep.tile([P, 1], F32, name="warm_in")
        warm_out = keep.tile([P, 1], F32, name="warm_out")
        nc.vector.memset(warm_in[:], 0.0)
        nc.scalar.activation(warm_out[:], warm_in[:], SIGMOID)

        picked_words, picked_scales = [], []
        for d in range(TAPS):
            ps = keep.tile([P, S], U8, name=f"picked_scales{d}", align_bytes=256)
            nc.vector.tensor_copy(ps[:], table_scales[:].indirect(lists[d][:]))
            picked_scales.append(ps)

        def gather_words(d, tag):
            pw = keep.tile([P, S], U32, name=f"picked_words{d}", tag=tag, align_bytes=256)
            nc.vector.tensor_copy(pw[:], table_words[:].indirect(lists[d][:]))
            picked_words.append(pw)

        for d in range(2):
            gather_words(d, f"picked_words{d}")

        staged, codes, scales = {}, {}, {}
        for name in names:
            staged[name] = keep.tile([P, PACK, P, PACK], BF16, name=f"staged_{name}", tag=f"staged_{name}", align_bytes=256)
            codes[name] = keep.tile([P, N], U32, name=f"codes_{name}", align_bytes=256)
            scales[name] = keep.tile([P, N], U8, name=f"scales_{name}", align_bytes=256)

        def cast(copy, name, first, last):
            src = raw[name, 0][:].rearrange("p j (m i t) -> p m j i t", i=2, t=PACK)
            dst = staged[name][:].rearrange("p t (m i) j -> p m j i t", i=2)
            copy(out=dst[:, first // 2 : last // 2], in_=src[:, first // 2 : last // 2])

        def cast_shared(name, split):
            cast(on_v, name, 0, split)
            cast(on_s, name, split, P)

        def cast_pair(copy, name, h, u, columns=slice(None)):
            src = raw[name, h][:].rearrange("p j (m u e) -> p u m j e", u=2, e=2)
            dst = staged[name][:].rearrange("p (u e) (h m) j -> p h u m j e", u=2, h=pieces[name])
            copy(out=dst[:, h, u, columns], in_=src[:, u, columns])

        def quantise(name, first, last):
            nc.vector.quantize_mx(
                out=codes[name][:, first:last].bitcast(FP8X4),
                scales=scales[name][:, first:last],
                in_=staged[name][:].rearrange("p t m j -> p (t m j)")[:, PACK * first : PACK * last],
            )

        def multiply(out, name, d, u, e, frames, start, stop):
            cols = slice((2 * u + e) * P, (2 * u + e + 1) * P)
            nc.tensor.matmul_mx(
                out=out,
                lhsT=codes[name][:, cols].bitcast(FP8X4),
                lhsT_scale=scales[name][:, cols],
                rhs=picked_words[d][:, frames].bitcast(FP8X4),
                rhs_scale=picked_scales[d][:, frames],
                start=start,
                stop=stop,
            )

        def multiply_half(acc, name, d, u, h):
            for e in range(2):
                alone = acc is f_acc and (h, u) == (0, 0)
                multiply(
                    acc[h][u][e], name, d, u, e, slice(h * HALF, (h + 1) * HALF),
                    d == 0 and (e == 0 or alone), d == TAPS - 1 and (e == 1 or alone),
                )

        def multiply_all(acc, name, d, pairs=(0, 1)):
            for h in range(2):
                for u in pairs:
                    multiply_half(acc, name, d, u, h)

        def gates(banks, tag):
            tile = keep.tile([P, len(banks), 2, HALF], F32, name=f"gate_after_{tag}", tag=tag, align_bytes=256)
            for i, (h, u) in enumerate(banks):
                nc.scalar.activation(tile[:, i, :, :], g_bank[h][u][:], SIGMOID)
                gate[h, u] = tile[:, i, :, :]

        on_s, on_v = nc.scalar.copy, nc.vector.tensor_copy
        g_bank = [[psum.tile([P, 2, HALF], F32, name=f"g_bank{h}_{u}", tag=f"g_bank{h}_{u}") for u in range(2)] for h in range(2)]
        f_bank = [[psum.tile([P, 2, HALF], F32, name=f"f_bank{h}_{u}") for u in range(2)] for h in range(2)]
        g_acc = [[[g_bank[h][u][:, e, :] for e in range(2)] for u in range(2)] for h in range(2)]
        f_acc = [[[f_bank[h][u][:, e, :] for e in range(2)] for u in range(2)] for h in range(2)]

        for d in range(TAPS):
            name = f"v{d}"
            if d < TAPS - 1:
                cast(on_s, name, 0, P)
            else:
                cast_shared(name, V2_SPLIT)
            quantise(name, 0, N)
            multiply_all(g_acc, name, d)
            if d == 0:
                gather_words(2, "staged_v0")
        cast_shared("w0", P // 2)
        gate = {}
        gates([(0, 0)], "raw_w0_0")
        f_second = psum.tile([P, HALF], F32, name="f_second", tag="g_bank0_0")
        f_acc[0][0][1] = f_second[:]
        quantise("w0", 0, N)
        multiply_all(f_acc, "w0", 0)
        cast_pair(on_v, "w1", 0, 1)
        cast_pair(on_v, "w1", 0, 0, slice(0, W1_EXTRA))
        cast_pair(on_s, "w1", 0, 0, slice(W1_EXTRA, P))
        for u in (1, 0):
            quantise("w1", 2 * u * P, 2 * (u + 1) * P)
            multiply_all(f_acc, "w1", 1, (u,))
        for u in range(2):
            cast_pair(on_s, "w2", 0, u)
        for t in range(2):
            quantise("w2", t * P, t * P + P // 2)
        cast_pair(on_v, "w2", 1, 0)
        cast_pair(on_v, "w2", 1, 1, slice(0, LAST_EXTRA))
        cast_pair(on_s, "w2", 1, 1, slice(LAST_EXTRA, P // 2))
        for t in range(2, PACK):
            quantise("w2", t * P, t * P + P // 2)
        for t in range(PACK):
            quantise("w2", t * P + P // 2, (t + 1) * P)
        gates([(0, 1), (1, 0), (1, 1)], "raw_w2_1")
        multiply_all(f_acc, "w2", TAPS - 1)

        y_codes = keep.tile([P, S], U32, name="y_codes", align_bytes=256)
        y_scales = keep.tile([P, S], U8, name="y_scales", align_bytes=256)
        out_rows = out_0.rearrange("(p t) j -> p t j", t=PACK)
        out_words = out_1[0].rearrange("p c r -> p (c r)").bitcast(I32)
        ys = [keep.tile([P, PACK, HALF], F32, name=f"y{h}", align_bytes=256) for h in range(2)]
        rounded = [keep.tile([P, HALF, PACK], BF16, name=f"rounded{h}", align_bytes=256) for h in range(2)]

        def store(h, tiles):
            nc.sync.dma_start(out=out_rows[:, tiles, h * HALF : (h + 1) * HALF], in_=ys[h][:, tiles, :])

        def gate_pair(h, u, first, last):
            nc.vector.tensor_tensor(
                ys[h][:, 2 * u : 2 * u + 2, first:last], f_bank[h][u][:, :, first:last], gate[h, u][:, :, first:last], MULT
            )

        def round_frames(copy, h, first, last):
            copy(
                out=rounded[h][:, first:last, :].rearrange("p (c i) t -> p c t i", i=4),
                in_=ys[h][:, :, first:last].rearrange("p t (c i) -> p c t i", i=4),
            )

        def finish(h, first, last):
            cols = slice(h * HALF + first, h * HALF + last)
            nc.vector.quantize_mx(
                out=y_codes[:, cols].bitcast(FP8X4),
                scales=y_scales[:, cols],
                in_=rounded[h][:, first:last, :].rearrange("p c t -> p (c t)"),
            )

        for e in range(2):
            nc.vector.tensor_tensor(ys[0][:, e, :], f_acc[0][0][e], gate[0, 0][:, e, :], MULT)
        store(0, slice(0, 2))
        gate_pair(0, 1, 0, QUARTER)
        gate_pair(0, 1, QUARTER, HALF)
        store(0, slice(2, 4))
        round_frames(on_s, 0, 0, QUARTER)
        round_frames(on_s, 0, QUARTER, HALF)
        gate_pair(1, 0, 0, HALF)
        store(1, slice(0, 2))
        gate_pair(1, 1, 0, QUARTER)
        gate_pair(1, 1, QUARTER, HALF)
        store(1, slice(2, 4))
        round_frames(on_v, 1, 0, QUARTER)
        round_frames(on_v, 1, QUARTER, ON_VECTOR)
        round_frames(on_s, 1, ON_VECTOR, HALF)
        for h in range(2):
            finish(h, 0, HALF)
            cols = slice(h * HALF, (h + 1) * HALF)
            nc.sync.dma_start(out=out_words[:, cols], in_=y_codes[:, cols].bitcast(I32))
        for q in range(4):
            queue = nc.sync if q % 2 == 0 else nc.scalar
            queue.dma_start(
                out=out_2[0, 4 * q : 4 * q + 4, :].bitcast(I32),
                in_=y_scales[32 * q : 32 * q + 4, :].bitcast(I32),
            )
